import numpy as np
import ml_dtypes


def mxq(x, axis, fmt="e4m3"):
    dtype, down = {"e4m3": (ml_dtypes.float8_e4m3fn, 7), "e5m2": (ml_dtypes.float8_e5m2, 14)}[fmt]
    v = np.moveaxis(np.asarray(x, np.float32).astype(ml_dtypes.bfloat16).astype(np.float64), axis, -1)
    blocks = v.reshape(v.shape[:-1] + (-1, 32))
    amax = np.abs(blocks).max(-1, keepdims=True)
    byte = np.maximum(np.where(amax > 0, np.frexp(amax)[1] - 1 + 127, 0) - down, 1)
    scale = np.exp2(byte - 127.0)
    codes = (blocks / scale).astype(np.float32).astype(dtype).astype(np.float64)
    return np.moveaxis((codes * scale).reshape(v.shape), -1, axis)


WIDE = False


def mx_kscale(k):
    if not WIDE:
        return np.ones(k)
    levels = np.array([10, -10, 5, -5, 0])
    if k % 512:
        return np.exp2(np.random.permutation(np.resize(levels, k // 32))).repeat(32)
    a = np.empty((k // 512, 16))
    for p in range(k // 512):
        a[p, :8] = np.random.permutation(np.resize(levels, 8))
        for g in range(8):
            far = levels[np.abs(levels - a[p, g]) >= 10]
            a[p, g + 8] = far[np.random.randint(len(far))]
    return np.exp2(a.ravel()).repeat(32)


def f64(x):
    return np.asarray(x).astype(np.float64)


def striped8(idx):
    return np.concatenate([v.reshape(-1, 16).T for v in idx]).astype(np.uint16)


def unstriped8(offs):
    return np.stack([offs[16 * g:16 * g + 16].T.reshape(-1) for g in range(8)]).astype(np.int64)


E2M1 = np.array([0.0, 0.5, 1.0, 1.5, 2.0, 3.0, 4.0, 6.0, -0.0, -0.5, -1.0, -1.5, -2.0, -3.0, -4.0, -6.0])


def pack_weight(w, fmt):
    k, n = w.shape
    w = f64(np.asarray(w, np.float32).astype(ml_dtypes.bfloat16)).reshape(k // 32, 32, n)
    amax = np.abs(w).max(1)
    if fmt == "e4m3":
        byte = np.frexp(amax)[1] - 1 + 127 - 7
    else:
        mant, ex = np.frexp(amax / 6.0)
        byte = np.where(mant > 0.5, ex, ex - 1) + 127
    byte = np.clip(np.where(amax > 0, byte, 1), 1, 254)
    scaled = (w * np.exp2(127.0 - byte)[:, None, :]).reshape(k, n).astype(np.float32)
    by_word = np.ascontiguousarray(scaled.reshape(k // 512, 128, 4, n).transpose(0, 1, 3, 2))
    if fmt == "e4m3":
        words = by_word.astype(ml_dtypes.float8_e4m3fn).view(np.uint8)
    else:
        c = by_word.astype(ml_dtypes.float4_e2m1fn).view(np.uint8) & 0xF
        words = (c[..., 0::2] | (c[..., 1::2] << 4)).reshape(k // 512, 128, 2 * n)
    return np.ascontiguousarray(words), np.ascontiguousarray(byte.astype(np.uint8).reshape(k // 512, 16, n))


def unpack_weight(words, scales, fmt):
    g, _, n = scales.shape
    words = np.ascontiguousarray(words).reshape(g, 128, n, -1)
    if fmt == "e4m3":
        vals = words.view(ml_dtypes.float8_e4m3fn).astype(np.float64)
    else:
        nib = np.empty((g, 128, n, 4), np.uint8)
        nib[..., 0::2] = words & 0xF
        nib[..., 1::2] = words >> 4
        vals = E2M1[nib]
    vals = vals * np.repeat(np.exp2(scales.astype(np.float64) - 127.0), 8, axis=1)[..., None]
    return vals.transpose(0, 1, 3, 2).reshape(g * 512, n)


def gelu(v):
    return 0.5 * v * (1.0 + np.tanh(np.sqrt(2.0 / np.pi) * (v + 0.044715 * v**3)))


K, M, T, S = 1536, 1024, 1024, 512


def setup_inputs():
    n = np.random.standard_normal
    s = mx_kscale(K)[:, None]
    w = n((K, M)) / np.sqrt(K) / s
    w4 = pack_weight(w, "e2m1")
    rest = w - unpack_weight(*w4, "e2m1")
    p_r8 = pack_weight(rest, "e4m3")
    return {
        "xT": (n((K, T)) * s).astype(np.float32),
        "w4_words": w4[0],
        "w4_scales": w4[1],
        "r8_words": p_r8[0],
        "r8_scales": p_r8[1],
        "wgt": np.repeat(np.random.uniform(0.5, 2.0, (8, S)), 16, axis=0).astype(np.float32),
        "b": (0.3 * n(1024)).astype(np.float32),
        "offs": striped8(np.stack([np.random.permutation(T)[:S] for _ in range(8)])),
    }


def reference(xT, w4_words, w4_scales, r8_words, r8_scales, wgt, b, offs):
    idx = unstriped8(offs)
    group = np.arange(K) % 512 // 64
    xg = f64(wgt)[np.arange(K) // 4 % 128] * f64(xT)[np.arange(K)[:, None], idx[group]]
    xT_ = mxq(xg, 0, "e4m3")
    w4_ = unpack_weight(w4_words, w4_scales, "e2m1")
    r8_ = unpack_weight(r8_words, r8_scales, "e4m3")
    y = xT_.T @ w4_ + xT_.T @ r8_
    return gelu(y + f64(b)[None, :])

@@ -1,0 +1,203 @@
+from contextlib import ExitStack
+
+import concourse.mybir as mybir
+from concourse.masks import make_identity
+
+K, M, T, S = 1536, 1024, 1024, 512
+FLOPS = 2 * 2 * K * M * S
+
+F32 = mybir.dt.float32
+BF16 = mybir.dt.bfloat16
+I32 = mybir.dt.int32
+U32 = mybir.dt.uint32
+U16 = mybir.dt.uint16
+U8 = mybir.dt.uint8
+FP8X4 = mybir.dt.float8_e4m3fn_x4
+FP4X4 = mybir.dt.float4_e2m1fn_x4
+ADD = mybir.AluOpType.add
+MULT = mybir.AluOpType.mult
+GELU = mybir.ActivationFunctionType.Gelu_apprx_tanh
+
+P = 128
+PACK = 4
+PASSES = K // (P * PACK)
+HALF = 512
+HALVES = M // HALF
+J_TILES = S // P
+MAIN = 384
+
+
+def tile_list_heads_tm_gelu_kernel(
+    tc, xT, w4_words, w4_scales, r8_words, r8_scales, wgt, b, offs, out
+):
+    nc = tc.nc
+    with ExitStack() as ctx:
+        held = ctx.enter_context(tc.tile_pool(name="held", bufs=1))
+        stage = ctx.enter_context(tc.tile_pool(name="stage", bufs=4))
+        psum = ctx.enter_context(tc.psum_pool(name="psum", bufs=1))
+
+        offsets = held.tile([P, S // 16], U16, name="offsets")
+        nc.sync.dma_start(offsets[:], offs)
+        factors = held.tile([P, S], F32, name="factors")
+        nc.sync.dma_start(factors[:], wgt)
+
+        w4_planes = held.tile([P, PASSES, M], U8, name="w4_planes", align_bytes=64)
+        r8_planes = held.tile([P, PASSES, M], U8, name="r8_planes", align_bytes=64)
+        nc.vector.memset(w4_planes[:].bitcast(I32), 0)
+        nc.vector.memset(r8_planes[:].bitcast(I32), 0)
+
+        warm = held.tile([P, 1], F32, name="warm")
+        nc.vector.memset(warm[:], 0.0)
+        nc.scalar.activation(warm[:], warm[:], GELU)
+
+        ident = held.tile([P, P], F32, name="ident")
+        make_identity(nc, ident[:])
+
+        def load_scales(queue, all_planes, scales, q):
+            queue.dma_start(
+                out=all_planes[32 * q : 32 * q + 4, :, :].bitcast(I32),
+                in_=scales[:, 4 * q : 4 * q + 4, :].rearrange("a q n -> q a n").bitcast(I32),
+            )
+
+        for q in range(4):
+            load_scales(nc.gpsimd, w4_planes, w4_scales, q)
+
+        x = {}
+        r8 = []
+        w4 = []
+
+        def load_x(a, i):
+            plane = held.tile([P, T], F32, name="x%d_%d" % (a, i))
+            rows = xT[512 * a : 512 * (a + 1), :].rearrange("(p i) t -> p i t", i=PACK)
+            nc.sync.dma_start(out=plane[:], in_=rows[:, i, :])
+            x[a, i] = plane
+
+        def load_w(a, pieces):
+            r8_tile = held.tile([P, M], U32, name="r8_%d" % a, align_bytes=64)
+            w4_tile = held.tile([P, 2 * M], U8, name="w4_%d" % a, align_bytes=64)
+            r8.append(r8_tile)
+            w4.append(w4_tile)
+            for h in range(pieces):
+                n = M // pieces
+                nc.sync.dma_start(
+                    out=w4_tile[:, 2 * n * h : 2 * n * (h + 1)].bitcast(I32),
+                    in_=w4_words[a][:, 2 * n * h : 2 * n * (h + 1)].bitcast(I32),
+                )
+                nc.sync.dma_start(
+                    out=r8_tile[:, n * h : n * (h + 1)].bitcast(I32),
+                    in_=r8_words[a].rearrange("p n t -> p (n t)")[:, 4 * n * h : 4 * n * (h + 1)].bitcast(I32),
+                )
+
+        for a in range(PASSES):
+            for i in range(PACK):
+                load_x(a, i)
+                if a == 0:
+                    load_scales(nc.sync, r8_planes, r8_scales, i)
+            if a == 0:
+                b_cols = held.tile([P, M // P], F32, name="b_cols")
+                nc.sync.dma_start(out=b_cols[:], in_=b.rearrange("(p c) -> p c", c=M // P))
+            load_w(a, 2 if a == PASSES - 1 else 1)
+
+        banks = {}
+        for jt in range(J_TILES):
+            for h in range(HALVES):
+                banks[jt, h] = psum.tile([P, HALF], F32, name="bank%d_%d" % (jt, h))
+
+        bias = held.tile([P, M], F32, name="bias")
+        for g in range(2):
+            bank = banks[J_TILES - 1, g]
+            for c in range(4):
+                nc.tensor.transpose(
+                    bank[:, P * c : P * (c + 1)],
+                    b_cols[:, 4 * g + c : 4 * g + c + 1].to_broadcast([P, P]),
+                    ident[:],
+                )
+            nc.scalar.copy(
+                out=bias[:].rearrange("j (p c) -> j p c", c=8)[:, :, 4 * g : 4 * g + 4],
+                in_=bank[:].rearrange("j (c p) -> j p c", c=4),
+            )
+
+        picked = []
+        grouped = []
+        codes = []
+        planes = []
+        for a in range(PASSES):
+            picked.append(held.tile([P, PACK, S], F32, name="picked%d" % a))
+            grouped.append(held.tile([P, S, PACK], BF16, name="grouped%d" % a, align_bytes=64))
+            codes.append(held.tile([P, S], U32, name="codes%d" % a, align_bytes=64))
+            planes.append(held.tile([P, S], U8, name="planes%d" % a, align_bytes=64))
+
+        def gather(a, i, j0, j1):
+            nc.vector.tensor_tensor(
+                picked[a][:, i, j0:j1],
+                x[a, i][:].indirect(offsets[:, j0 // 16 : j1 // 16]),
+                factors[:, j0:j1],
+                MULT,
+            )
+
+        def interleave(a, j0, j1):
+            nc.scalar.copy(
+                out=grouped[a][:, j0:j1, :],
+                in_=picked[a][:, :, j0:j1].rearrange("p i j -> p j i"),
+            )
+
+        def quantize(a, j0, j1):
+            nc.vector.quantize_mx(
+                out=codes[a][:, j0:j1].bitcast(FP8X4),
+                scales=planes[a][:, j0:j1],
+                in_=grouped[a][:, j0:j1, :].rearrange("p j i -> p (j i)"),
+            )
+
+        def multiply(a, jt, h):
+            j = slice(P * jt, P * (jt + 1))
+            n = slice(HALF * h, HALF * (h + 1))
+            nc.tensor.matmul_mx(
+                out=banks[jt, h][:],
+                lhsT=codes[a][:, j].bitcast(FP8X4),
+                lhsT_scale=planes[a][:, j],
+                rhs=w4[a][:, 2 * HALF * h : 2 * HALF * (h + 1)].bitcast(FP4X4),
+                rhs_scale=w4_planes[:, a, n],
+                start=(a == 0),
+                stop=False,
+            )
+            nc.tensor.matmul_mx(
+                out=banks[jt, h][:],
+                lhsT=codes[a][:, j].bitcast(FP8X4),
+                lhsT_scale=planes[a][:, j],
+                rhs=r8[a][:, n].bitcast(FP8X4),
+                rhs_scale=r8_planes[:, a, n],
+                start=False,
+                stop=(a == PASSES - 1),
+            )
+
+        def finish(jt, h):
+            n = slice(HALF * h, HALF * (h + 1))
+            y = stage.tile([P, HALF], F32, name="y")
+            nc.vector.tensor_tensor(y[:], banks[jt, h][:], bias[:, n], ADD)
+            o = stage.tile([P, HALF], F32, name="o")
+            nc.scalar.activation(o[:], y[:], GELU)
+            nc.sync.dma_start(out=out[P * jt : P * (jt + 1), n], in_=o[:])
+
+        main_tiles = range(MAIN // P)
+        for a in range(PASSES):
+            for i in range(PACK):
+                gather(a, i, 0, MAIN)
+            interleave(a, 0, 256)
+            quantize(a, 0, 256)
+            interleave(a, 256, MAIN)
+            quantize(a, 256, MAIN)
+            for h in range(HALVES):
+                for jt in main_tiles:
+                    multiply(a, jt, h)
+        for h in range(HALVES):
+            for jt in main_tiles:
+                finish(jt, h)
+        for a in range(PASSES):
+            for i in range(PACK):
+                gather(a, i, MAIN, S)
+            interleave(a, MAIN, S)
+            quantize(a, MAIN, S)
+            for h in range(HALVES):
+                multiply(a, J_TILES - 1, h)
+        for h in range(HALVES):
+            finish(J_TILES - 1, h)

@@ -33,7 +33,7 @@ def tile_list_heads_tm_gelu_kernel(
     nc = tc.nc
     with ExitStack() as ctx:
         held = ctx.enter_context(tc.tile_pool(name="held", bufs=1))
-        stage = ctx.enter_context(tc.tile_pool(name="stage", bufs=4))
+        stage = ctx.enter_context(tc.tile_pool(name="stage", bufs=8))
         psum = ctx.enter_context(tc.psum_pool(name="psum", bufs=1))
 
         offsets = held.tile([P, S // 16], U16, name="offsets")
@@ -46,12 +46,12 @@ def tile_list_heads_tm_gelu_kernel(
         nc.vector.memset(w4_planes[:].bitcast(I32), 0)
         nc.vector.memset(r8_planes[:].bitcast(I32), 0)
 
+        b_cols = held.tile([P, M // P], F32, name="b_cols")
+        nc.scalar.dma_start(out=b_cols[:], in_=b.rearrange("(p c) -> p c", c=M // P))
+
         warm = held.tile([P, 1], F32, name="warm")
         nc.vector.memset(warm[:], 0.0)
         nc.scalar.activation(warm[:], warm[:], GELU)
-
-        ident = held.tile([P, P], F32, name="ident")
-        make_identity(nc, ident[:])
 
         def load_scales(queue, all_planes, scales, q):
             queue.dma_start(
@@ -59,8 +59,8 @@ def tile_list_heads_tm_gelu_kernel(
                 in_=scales[:, 4 * q : 4 * q + 4, :].rearrange("a q n -> q a n").bitcast(I32),
             )
 
-        for q in range(4):
-            load_scales(nc.gpsimd, w4_planes, w4_scales, q)
+        ident = held.tile([P, P], F32, name="ident")
+        make_identity(nc, ident[:])
 
         x = {}
         r8 = []
@@ -79,6 +79,9 @@ def tile_list_heads_tm_gelu_kernel(
             w4.append(w4_tile)
             for h in range(pieces):
                 n = M // pieces
+                if a == 0:
+                    load_scales(nc.sync, r8_planes, r8_scales, 0)
+                    load_scales(nc.sync, r8_planes, r8_scales, 1)
                 nc.sync.dma_start(
                     out=w4_tile[:, 2 * n * h : 2 * n * (h + 1)].bitcast(I32),
                     in_=w4_words[a][:, 2 * n * h : 2 * n * (h + 1)].bitcast(I32),
@@ -87,16 +90,16 @@ def tile_list_heads_tm_gelu_kernel(
                     out=r8_tile[:, n * h : n * (h + 1)].bitcast(I32),
                     in_=r8_words[a].rearrange("p n t -> p (n t)")[:, 4 * n * h : 4 * n * (h + 1)].bitcast(I32),
                 )
+                if a == 0:
+                    load_scales(nc.sync, r8_planes, r8_scales, 2)
+                    load_scales(nc.sync, r8_planes, r8_scales, 3)
 
         for a in range(PASSES):
             for i in range(PACK):
                 load_x(a, i)
                 if a == 0:
-                    load_scales(nc.sync, r8_planes, r8_scales, i)
-            if a == 0:
-                b_cols = held.tile([P, M // P], F32, name="b_cols")
-                nc.sync.dma_start(out=b_cols[:], in_=b.rearrange("(p c) -> p c", c=M // P))
-            load_w(a, 2 if a == PASSES - 1 else 1)
+                    load_scales(nc.sync, w4_planes, w4_scales, i)
+            load_w(a, 1)
 
         banks = {}
         for jt in range(J_TILES):
@@ -135,10 +138,10 @@ def tile_list_heads_tm_gelu_kernel(
                 MULT,
             )
 
-        def interleave(a, j0, j1):
+        def interleave(a, j0, j1, i0=0, i1=PACK):
             nc.scalar.copy(
-                out=grouped[a][:, j0:j1, :],
-                in_=picked[a][:, :, j0:j1].rearrange("p i j -> p j i"),
+                out=grouped[a][:, j0:j1, i0:i1].rearrange("p (c u) i -> p c i u", u=4),
+                in_=picked[a][:, i0:i1, j0:j1].rearrange("p i (c u) -> p c i u", u=4),
             )
 
         def quantize(a, j0, j1):
@@ -173,31 +176,58 @@ def tile_list_heads_tm_gelu_kernel(
         def finish(jt, h):
             n = slice(HALF * h, HALF * (h + 1))
             y = stage.tile([P, HALF], F32, name="y")
-            nc.vector.tensor_tensor(y[:], banks[jt, h][:], bias[:, n], ADD)
             o = stage.tile([P, HALF], F32, name="o")
-            nc.scalar.activation(o[:], y[:], GELU)
-            nc.sync.dma_start(out=out[P * jt : P * (jt + 1), n], in_=o[:])
+            pieces = 2 if (jt, h) == (J_TILES - 1, HALVES - 1) else 1
+            w = HALF // pieces
+            for c in range(0, HALF, w):
+                nc.vector.tensor_tensor(y[:, c : c + w], banks[jt, h][:, c : c + w], bias[:, HALF * h + c : HALF * h + c + w], ADD)
+                nc.scalar.activation(o[:, c : c + w], y[:, c : c + w], GELU)
+                nc.sync.dma_start(out=out[P * jt : P * (jt + 1), HALF * h + c : HALF * h + c + w], in_=o[:, c : c + w])
 
-        main_tiles = range(MAIN // P)
-        for a in range(PASSES):
-            for i in range(PACK):
-                gather(a, i, 0, MAIN)
-            interleave(a, 0, 256)
-            quantize(a, 0, 256)
-            interleave(a, 256, MAIN)
-            quantize(a, 256, MAIN)
+        def multiply_tiles(a, tiles):
             for h in range(HALVES):
-                for jt in main_tiles:
+                for jt in tiles:
                     multiply(a, jt, h)
-        for h in range(HALVES):
-            for jt in main_tiles:
-                finish(jt, h)
-        for a in range(PASSES):
-            for i in range(PACK):
-                gather(a, i, MAIN, S)
-            interleave(a, MAIN, S)
-            quantize(a, MAIN, S)
+
+        A = (0, 256)
+        B = (256, S)
+        for i in range(PACK):
+            gather(0, i, *A)
+            gather(0, i, *B)
+        interleave(0, *A)
+        interleave(0, *B)
+        for i in range(PACK):
+            gather(1, i, *A)
+            if i == 0:
+                quantize(0, 0, S)
+                multiply_tiles(0, range(J_TILES))
+            gather(1, i, *B)
+        interleave(1, *A)
+        interleave(1, *B)
+        gather(2, 0, *A)
+        quantize(1, *A)
+        multiply_tiles(1, (0, 1))
+        gather(2, 0, *B)
+        gather(2, 1, *A)
+        quantize(1, *B)
+        multiply_tiles(1, (2, 3))
+        gather(2, 1, *B)
+        interleave(2, *A, 0, 2)
+        interleave(2, *B, 0, 2)
+        gather(2, 2, *A)
+        gather(2, 2, *B)
+        gather(2, 3, 0, P)
+        interleave(2, 0, P, 2, 4)
+        gather(2, 3, P, S)
+        for jt in range(1, J_TILES):
+            interleave(2, P * jt, P * (jt + 1), 2, 4)
+        done = []
+        for jt in range(J_TILES):
+            quantize(2, P * jt, P * (jt + 1))
+            multiply_tiles(2, (jt,))
+            if jt == 2:
+                finish(0, 0)
+        for jt in range(J_TILES):
             for h in range(HALVES):
-                multiply(a, J_TILES - 1, h)
-        for h in range(HALVES):
-            finish(J_TILES - 1, h)
+                if (jt, h) != (0, 0):
+                    finish(jt, h)

@@ -39,7 +39,7 @@ def tile_list_heads_tm_gelu_kernel(
         offsets = held.tile([P, S // 16], U16, name="offsets")
         nc.sync.dma_start(offsets[:], offs)
         factors = held.tile([P, S], F32, name="factors")
-        nc.sync.dma_start(factors[:], wgt)
+        nc.sync.dma_start(factors[:, 0:256], wgt[:, 0:256])
 
         w4_planes = held.tile([P, PASSES, M], U8, name="w4_planes", align_bytes=64)
         r8_planes = held.tile([P, PASSES, M], U8, name="r8_planes", align_bytes=64)
@@ -97,6 +97,8 @@ def tile_list_heads_tm_gelu_kernel(
         for a in range(PASSES):
             for i in range(PACK):
                 load_x(a, i)
+                if a == 0 and i == 0:
+                    nc.sync.dma_start(factors[:, 256:S], wgt[:, 256:S])
                 if a == 0:
                     load_scales(nc.sync, w4_planes, w4_scales, i)
             load_w(a, 1)
@@ -191,43 +193,47 @@ def tile_list_heads_tm_gelu_kernel(
 
         A = (0, 256)
         B = (256, S)
-        for i in range(PACK):
-            gather(0, i, *A)
-            gather(0, i, *B)
-        interleave(0, *A)
-        interleave(0, *B)
-        for i in range(PACK):
-            gather(1, i, *A)
-            if i == 0:
-                quantize(0, 0, S)
-                multiply_tiles(0, range(J_TILES))
-            gather(1, i, *B)
-        interleave(1, *A)
-        interleave(1, *B)
-        gather(2, 0, *A)
+        for a in (0, 1):
+            for i in range(PACK):
+                gather(a, i, *A)
+                if i % 2 == 1:
+                    interleave(a, *A, i - 1, i + 1)
+                gather(a, i, *B)
+                if i % 2 == 1:
+                    interleave(a, *B, i - 1, i + 1)
+                if a == 1 and i == 0:
+                    quantize(0, *B)
+                    multiply_tiles(0, (2, 3))
+            if a == 0:
+                quantize(0, *A)
+                multiply_tiles(0, (0, 1))
+        gather(2, 0, 0, MAIN)
         quantize(1, *A)
         multiply_tiles(1, (0, 1))
-        gather(2, 0, *B)
-        gather(2, 1, *A)
+        gather(2, 1, 0, MAIN)
+        for jt in range(3):
+            interleave(2, P * jt, P * (jt + 1), 0, 2)
         quantize(1, *B)
         multiply_tiles(1, (2, 3))
-        gather(2, 1, *B)
-        interleave(2, *A, 0, 2)
-        interleave(2, *B, 0, 2)
-        gather(2, 2, *A)
-        gather(2, 2, *B)
-        gather(2, 3, 0, P)
-        interleave(2, 0, P, 2, 4)
-        gather(2, 3, P, S)
-        for jt in range(1, J_TILES):
+        gather(2, 2, 0, MAIN)
+        gather(2, 3, 0, MAIN)
+        for jt in range(3):
             interleave(2, P * jt, P * (jt + 1), 2, 4)
-        done = []
-        for jt in range(J_TILES):
+        gather(2, 0, MAIN, S)
+        gather(2, 1, MAIN, S)
+        interleave(2, MAIN, S, 0, 2)
+        quantize(2, 0, P)
+        multiply_tiles(2, (0,))
+        gather(2, 2, MAIN, S)
+        for jt in (1, 2):
             quantize(2, P * jt, P * (jt + 1))
             multiply_tiles(2, (jt,))
-            if jt == 2:
-                finish(0, 0)
-        for jt in range(J_TILES):
+        gather(2, 3, MAIN, S)
+        interleave(2, MAIN, S, 2, 4)
+        finish(0, 0)
+        finish(0, 1)
+        quantize(2, MAIN, S)
+        multiply_tiles(2, (3,))
+        for jt in range(1, J_TILES):
             for h in range(HALVES):
-                if (jt, h) != (0, 0):
-                    finish(jt, h)
+                finish(jt, h)

@@ -207,32 +207,33 @@ def tile_list_heads_tm_gelu_kernel(
             if a == 0:
                 quantize(0, *A)
                 multiply_tiles(0, (0, 1))
-        gather(2, 0, 0, MAIN)
+        gather(2, 0, *A)
         quantize(1, *A)
         multiply_tiles(1, (0, 1))
-        gather(2, 1, 0, MAIN)
-        for jt in range(3):
-            interleave(2, P * jt, P * (jt + 1), 0, 2)
+        gather(2, 1, *A)
+        interleave(2, *A, 0, 2)
         quantize(1, *B)
         multiply_tiles(1, (2, 3))
-        gather(2, 2, 0, MAIN)
-        gather(2, 3, 0, MAIN)
-        for jt in range(3):
+        gather(2, 2, *A)
+        gather(2, 3, *A)
+        for jt in (0, 1):
             interleave(2, P * jt, P * (jt + 1), 2, 4)
-        gather(2, 0, MAIN, S)
-        gather(2, 1, MAIN, S)
-        interleave(2, MAIN, S, 0, 2)
+        gather(2, 0, *B)
         quantize(2, 0, P)
         multiply_tiles(2, (0,))
-        gather(2, 2, MAIN, S)
-        for jt in (1, 2):
-            quantize(2, P * jt, P * (jt + 1))
-            multiply_tiles(2, (jt,))
-        gather(2, 3, MAIN, S)
-        interleave(2, MAIN, S, 2, 4)
+        gather(2, 1, *B)
+        interleave(2, *B, 0, 2)
+        quantize(2, P, 2 * P)
+        multiply_tiles(2, (1,))
+        gather(2, 2, *B)
+        gather(2, 3, *B)
+        for jt in (2, 3):
+            interleave(2, P * jt, P * (jt + 1), 2, 4)
         finish(0, 0)
+        quantize(2, 2 * P, 3 * P)
+        multiply_tiles(2, (2,))
         finish(0, 1)
-        quantize(2, MAIN, S)
+        quantize(2, 3 * P, S)
         multiply_tiles(2, (3,))
         for jt in range(1, J_TILES):
             for h in range(HALVES):

from contextlib import ExitStack

import concourse.mybir as mybir
from concourse.masks import make_identity

K, M, T, S = 1536, 1024, 1024, 512
FLOPS = 2 * 2 * K * M * S

F32 = mybir.dt.float32
BF16 = mybir.dt.bfloat16
I32 = mybir.dt.int32
U32 = mybir.dt.uint32
U16 = mybir.dt.uint16
U8 = mybir.dt.uint8
FP8X4 = mybir.dt.float8_e4m3fn_x4
FP4X4 = mybir.dt.float4_e2m1fn_x4
ADD = mybir.AluOpType.add
MULT = mybir.AluOpType.mult
GELU = mybir.ActivationFunctionType.Gelu_apprx_tanh

P = 128
PACK = 4
PASSES = K // (P * PACK)
HALF = 512
HALVES = M // HALF
J_TILES = S // P
MAIN = 384


def tile_list_heads_tm_gelu_kernel(
    tc, xT, w4_words, w4_scales, r8_words, r8_scales, wgt, b, offs, out
):
    nc = tc.nc
    with ExitStack() as ctx:
        held = ctx.enter_context(tc.tile_pool(name="held", bufs=1))
        stage = ctx.enter_context(tc.tile_pool(name="stage", bufs=8))
        psum = ctx.enter_context(tc.psum_pool(name="psum", bufs=1))

        offsets = held.tile([P, S // 16], U16, name="offsets")
        nc.sync.dma_start(offsets[:], offs)
        factors = held.tile([P, S], F32, name="factors")
        nc.sync.dma_start(factors[:, 0:256], wgt[:, 0:256])

        w4_planes = held.tile([P, PASSES, M], U8, name="w4_planes", align_bytes=64)
        r8_planes = held.tile([P, PASSES, M], U8, name="r8_planes", align_bytes=64)
        nc.vector.memset(w4_planes[:].bitcast(I32), 0)
        nc.vector.memset(r8_planes[:].bitcast(I32), 0)

        b_cols = held.tile([P, M // P], F32, name="b_cols")
        nc.scalar.dma_start(out=b_cols[:], in_=b.rearrange("(p c) -> p c", c=M // P))

        warm = held.tile([P, 1], F32, name="warm")
        nc.vector.memset(warm[:], 0.0)
        nc.scalar.activation(warm[:], warm[:], GELU)

        def load_scales(queue, all_planes, scales, q):
            queue.dma_start(
                out=all_planes[32 * q : 32 * q + 4, :, :].bitcast(I32),
                in_=scales[:, 4 * q : 4 * q + 4, :].rearrange("a q n -> q a n").bitcast(I32),
            )

        ident = held.tile([P, P], F32, name="ident")
        make_identity(nc, ident[:])

        x = {}
        r8 = []
        w4 = []

        def load_x(a, i):
            plane = held.tile([P, T], F32, name="x%d_%d" % (a, i))
            rows = xT[512 * a : 512 * (a + 1), :].rearrange("(p i) t -> p i t", i=PACK)
            nc.sync.dma_start(out=plane[:], in_=rows[:, i, :])
            x[a, i] = plane

        def load_w(a, pieces):
            r8_tile = held.tile([P, M], U32, name="r8_%d" % a, align_bytes=64)
            w4_tile = held.tile([P, 2 * M], U8, name="w4_%d" % a, align_bytes=64)
            r8.append(r8_tile)
            w4.append(w4_tile)
            for h in range(pieces):
                n = M // pieces
                if a == 0:
                    load_scales(nc.sync, r8_planes, r8_scales, 0)
                    load_scales(nc.sync, r8_planes, r8_scales, 1)
                nc.sync.dma_start(
                    out=w4_tile[:, 2 * n * h : 2 * n * (h + 1)].bitcast(I32),
                    in_=w4_words[a][:, 2 * n * h : 2 * n * (h + 1)].bitcast(I32),
                )
                nc.sync.dma_start(
                    out=r8_tile[:, n * h : n * (h + 1)].bitcast(I32),
                    in_=r8_words[a].rearrange("p n t -> p (n t)")[:, 4 * n * h : 4 * n * (h + 1)].bitcast(I32),
                )
                if a == 0:
                    load_scales(nc.sync, r8_planes, r8_scales, 2)
                    load_scales(nc.sync, r8_planes, r8_scales, 3)

        for a in range(PASSES):
            for i in range(PACK):
                load_x(a, i)
                if a == 0 and i == 0:
                    nc.sync.dma_start(factors[:, 256:S], wgt[:, 256:S])
                if a == 0:
                    load_scales(nc.sync, w4_planes, w4_scales, i)
            load_w(a, 1)

        banks = {}
        for jt in range(J_TILES):
            for h in range(HALVES):
                banks[jt, h] = psum.tile([P, HALF], F32, name="bank%d_%d" % (jt, h))

        bias = held.tile([P, M], F32, name="bias")
        for g in range(2):
            bank = banks[J_TILES - 1, g]
            for c in range(4):
                nc.tensor.transpose(
                    bank[:, P * c : P * (c + 1)],
                    b_cols[:, 4 * g + c : 4 * g + c + 1].to_broadcast([P, P]),
                    ident[:],
                )
            nc.scalar.copy(
                out=bias[:].rearrange("j (p c) -> j p c", c=8)[:, :, 4 * g : 4 * g + 4],
                in_=bank[:].rearrange("j (c p) -> j p c", c=4),
            )

        picked = []
        grouped = []
        codes = []
        planes = []
        for a in range(PASSES):
            picked.append(held.tile([P, PACK, S], F32, name="picked%d" % a))
            grouped.append(held.tile([P, S, PACK], BF16, name="grouped%d" % a, align_bytes=64))
            codes.append(held.tile([P, S], U32, name="codes%d" % a, align_bytes=64))
            planes.append(held.tile([P, S], U8, name="planes%d" % a, align_bytes=64))

        def gather(a, i, j0, j1):
            nc.vector.tensor_tensor(
                picked[a][:, i, j0:j1],
                x[a, i][:].indirect(offsets[:, j0 // 16 : j1 // 16]),
                factors[:, j0:j1],
                MULT,
            )

        def interleave(a, j0, j1, i0=0, i1=PACK):
            nc.scalar.copy(
                out=grouped[a][:, j0:j1, i0:i1].rearrange("p (c u) i -> p c i u", u=4),
                in_=picked[a][:, i0:i1, j0:j1].rearrange("p i (c u) -> p c i u", u=4),
            )

        def quantize(a, j0, j1):
            nc.vector.quantize_mx(
                out=codes[a][:, j0:j1].bitcast(FP8X4),
                scales=planes[a][:, j0:j1],
                in_=grouped[a][:, j0:j1, :].rearrange("p j i -> p (j i)"),
            )

        def multiply(a, jt, h):
            j = slice(P * jt, P * (jt + 1))
            n = slice(HALF * h, HALF * (h + 1))
            nc.tensor.matmul_mx(
                out=banks[jt, h][:],
                lhsT=codes[a][:, j].bitcast(FP8X4),
                lhsT_scale=planes[a][:, j],
                rhs=w4[a][:, 2 * HALF * h : 2 * HALF * (h + 1)].bitcast(FP4X4),
                rhs_scale=w4_planes[:, a, n],
                start=(a == 0),
                stop=False,
            )
            nc.tensor.matmul_mx(
                out=banks[jt, h][:],
                lhsT=codes[a][:, j].bitcast(FP8X4),
                lhsT_scale=planes[a][:, j],
                rhs=r8[a][:, n].bitcast(FP8X4),
                rhs_scale=r8_planes[:, a, n],
                start=False,
                stop=(a == PASSES - 1),
            )

        def finish(jt, h):
            n = slice(HALF * h, HALF * (h + 1))
            y = stage.tile([P, HALF], F32, name="y")
            o = stage.tile([P, HALF], F32, name="o")
            pieces = 2 if (jt, h) == (J_TILES - 1, HALVES - 1) else 1
            w = HALF // pieces
            for c in range(0, HALF, w):
                nc.vector.tensor_tensor(y[:, c : c + w], banks[jt, h][:, c : c + w], bias[:, HALF * h + c : HALF * h + c + w], ADD)
                nc.scalar.activation(o[:, c : c + w], y[:, c : c + w], GELU)
                nc.sync.dma_start(out=out[P * jt : P * (jt + 1), HALF * h + c : HALF * h + c + w], in_=o[:, c : c + w])

        def multiply_tiles(a, tiles):
            for h in range(HALVES):
                for jt in tiles:
                    multiply(a, jt, h)

        A = (0, 256)
        B = (256, S)
        for a in (0, 1):
            for i in range(PACK):
                gather(a, i, *A)
                if i % 2 == 1:
                    interleave(a, *A, i - 1, i + 1)
                gather(a, i, *B)
                if i % 2 == 1:
                    interleave(a, *B, i - 1, i + 1)
                if a == 1 and i == 0:
                    quantize(0, *B)
                    multiply_tiles(0, (2, 3))
            if a == 0:
                quantize(0, *A)
                multiply_tiles(0, (0, 1))
        gather(2, 0, *A)
        quantize(1, *A)
        multiply_tiles(1, (0, 1))
        gather(2, 1, *A)
        interleave(2, *A, 0, 2)
        quantize(1, *B)
        multiply_tiles(1, (2, 3))
        gather(2, 2, *A)
        gather(2, 3, *A)
        for jt in (0, 1):
            interleave(2, P * jt, P * (jt + 1), 2, 4)
        gather(2, 0, *B)
        quantize(2, 0, P)
        multiply_tiles(2, (0,))
        gather(2, 1, *B)
        interleave(2, *B, 0, 2)
        quantize(2, P, 2 * P)
        multiply_tiles(2, (1,))
        gather(2, 2, *B)
        gather(2, 3, *B)
        for jt in (2, 3):
            interleave(2, P * jt, P * (jt + 1), 2, 4)
        finish(0, 0)
        quantize(2, 2 * P, 3 * P)
        multiply_tiles(2, (2,))
        finish(0, 1)
        quantize(2, 3 * P, S)
        multiply_tiles(2, (3,))
        for jt in range(1, J_TILES):
            for h in range(HALVES):
                finish(jt, h)
